import numpy as np
import ml_dtypes


def mxq(x, axis, fmt="e4m3"):
    dtype, down = {"e4m3": (ml_dtypes.float8_e4m3fn, 7), "e5m2": (ml_dtypes.float8_e5m2, 14)}[fmt]
    v = np.moveaxis(np.asarray(x, np.float32).astype(ml_dtypes.bfloat16).astype(np.float64), axis, -1)
    blocks = v.reshape(v.shape[:-1] + (-1, 32))
    amax = np.abs(blocks).max(-1, keepdims=True)
    byte = np.maximum(np.where(amax > 0, np.frexp(amax)[1] - 1 + 127, 0) - down, 1)
    scale = np.exp2(byte - 127.0)
    codes = (blocks / scale).astype(np.float32).astype(dtype).astype(np.float64)
    return np.moveaxis((codes * scale).reshape(v.shape), -1, axis)


WIDE = False


def mx_kscale(k):
    if not WIDE:
        return np.ones(k)
    levels = np.array([10, -10, 5, -5, 0])
    if k % 512:
        return np.exp2(np.random.permutation(np.resize(levels, k // 32))).repeat(32)
    a = np.empty((k // 512, 16))
    for p in range(k // 512):
        a[p, :8] = np.random.permutation(np.resize(levels, 8))
        for g in range(8):
            far = levels[np.abs(levels - a[p, g]) >= 10]
            a[p, g + 8] = far[np.random.randint(len(far))]
    return np.exp2(a.ravel()).repeat(32)


def f64(x):
    return np.asarray(x).astype(np.float64)


def striped(idx):
    return np.tile(np.asarray(idx).reshape(-1, 16).T, (8, 1)).astype(np.uint16)


def unstriped(offs):
    return offs[:16].T.reshape(-1).astype(np.int64)


E2M1 = np.array([0.0, 0.5, 1.0, 1.5, 2.0, 3.0, 4.0, 6.0, -0.0, -0.5, -1.0, -1.5, -2.0, -3.0, -4.0, -6.0])


def pack_weight(w, fmt):
    k, n = w.shape
    w = f64(np.asarray(w, np.float32).astype(ml_dtypes.bfloat16)).reshape(k // 32, 32, n)
    amax = np.abs(w).max(1)
    if fmt == "e4m3":
        byte = np.frexp(amax)[1] - 1 + 127 - 7
    else:
        mant, ex = np.frexp(amax / 6.0)
        byte = np.where(mant > 0.5, ex, ex - 1) + 127
    byte = np.clip(np.where(amax > 0, byte, 1), 1, 254)
    scaled = (w * np.exp2(127.0 - byte)[:, None, :]).reshape(k, n).astype(np.float32)
    by_word = np.ascontiguousarray(scaled.reshape(k // 512, 128, 4, n).transpose(0, 1, 3, 2))
    if fmt == "e4m3":
        words = by_word.astype(ml_dtypes.float8_e4m3fn).view(np.uint8)
    else:
        c = by_word.astype(ml_dtypes.float4_e2m1fn).view(np.uint8) & 0xF
        words = (c[..., 0::2] | (c[..., 1::2] << 4)).reshape(k // 512, 128, 2 * n)
    return np.ascontiguousarray(words), np.ascontiguousarray(byte.astype(np.uint8).reshape(k // 512, 16, n))


def unpack_weight(words, scales, fmt):
    g, _, n = scales.shape
    words = np.ascontiguousarray(words).reshape(g, 128, n, -1)
    if fmt == "e4m3":
        vals = words.view(ml_dtypes.float8_e4m3fn).astype(np.float64)
    else:
        nib = np.empty((g, 128, n, 4), np.uint8)
        nib[..., 0::2] = words & 0xF
        nib[..., 1::2] = words >> 4
        vals = E2M1[nib]
    vals = vals * np.repeat(np.exp2(scales.astype(np.float64) - 127.0), 8, axis=1)[..., None]
    return vals.transpose(0, 1, 3, 2).reshape(g * 512, n)


def bf(x):
    return np.asarray(x, np.float32).astype(ml_dtypes.bfloat16)


def planes(Y):
    r, m = Y.shape
    b = f64(bf(Y)).reshape(r // 32, 32, m)
    amax = np.abs(b).max(1)
    byte = np.clip(np.where(amax > 0, np.frexp(amax)[1] - 1 + 127 - 7, 1), 1, 254)
    codes = (b * np.exp2(127.0 - byte)[:, None, :]).reshape(r, m).astype(np.float32).astype(ml_dtypes.float8_e4m3fn).view(np.uint8)
    words = codes.reshape(r // 512, 128, 4, m).transpose(0, 1, 3, 2)
    return np.ascontiguousarray(words), np.ascontiguousarray(byte.astype(np.uint8).reshape(r // 512, 16, m))


D, T, I, Q, E, U, K = 512, 2048, 512, 256, 512, 1024, 32


def setup_inputs():
    n = np.random.standard_normal
    idx = np.random.permutation(T)[:I]
    idx2 = np.random.permutation(U)[:I]
    fd = mx_kscale(D)
    fi = mx_kscale(I)
    ti = np.ones(T)
    ti[idx] = fi
    keysp = pack_weight(n((D, T)) / fd[:, None], "e2m1")
    return {
        "query": (n((D, Q)) * 0.585 / np.sqrt(D) * fd[:, None]).astype(np.float32),
        "keys_words": keysp[0],
        "keys_scales": keysp[1],
        "concepts": (n((D, U)) / fd[:, None]).astype(np.float32),
        "part": np.tile(np.random.uniform(0.2, 1.0, T), (128, 1)).astype(np.float32),
        "lam": (np.random.uniform(0.7, 1.4, (Q, 1))).astype(np.float32),
        "sres": (np.random.uniform(1.0, 8.0, (I, 1))).astype(np.float32),
        "os": (np.random.uniform(4.0, 16.0, (1, I)) * fi).astype(np.float32),
        "vals": (n((E, T)) / ti).astype(np.float32),
        "memq": (np.random.uniform(0.3, 1.0, (1, Q))).astype(np.float32),
        "offs": striped(idx),
        "offs2": striped(idx2),
    }


def reference(query, keys_words, keys_scales, concepts, part, lam, sres, os, vals, memq, offs, offs2):
    idx = unstriped(offs)
    idx2 = unstriped(offs2)
    keysu = unpack_weight(keys_words, keys_scales, "e2m1")
    queryq = mxq(f64(query), 0, "e4m3")
    keysidxg = keysu[:, idx]
    a = queryq.T @ keysidxg
    conceptsidx2q = mxq(f64(concepts)[:, idx2], 0, "e4m3")
    b = queryq.T @ conceptsidx2q
    s = (a - b * f64(part)[:1][:, idx]) * f64(lam)
    p = np.exp(s)
    ptt = p.T
    rg = ptt.reshape(I, K, Q // K).sum(axis=2)
    rv0 = 1.0 / (rg + f64(sres))
    rr = np.repeat(rv0, Q // K, axis=1)
    w0 = ptt * rr
    w = w0.T
    wo1 = w * f64(os)
    wt1 = wo1.T
    vt1 = f64(vals)[:, idx].T
    vt1q = mxq(vt1, 0, "e4m3")
    wt1q = mxq(wt1, 0, "e4m3")
    o = vt1q.T @ wt1q
    o1 = np.pad(o, ((0, 0), (1, 0)))[:, :Q]
    y = o - o1 * f64(memq)
    words, scales = planes(y)
    return y, words, scales

@@ -1,0 +1,226 @@
+from contextlib import ExitStack
+
+import concourse.mybir as mybir
+from concourse.masks import make_identity
+
+D, T, I, Q, E, U, GROUP = 512, 2048, 512, 256, 512, 1024, 8
+FLOPS = 2 * D * Q * I * 2 + 2 * I * E * Q
+
+F32 = mybir.dt.float32
+BF16 = mybir.dt.bfloat16
+I32 = mybir.dt.int32
+U32 = mybir.dt.uint32
+U16 = mybir.dt.uint16
+U8 = mybir.dt.uint8
+FP8X4 = mybir.dt.float8_e4m3fn_x4
+FP4X4 = mybir.dt.float4_e2m1fn_x4
+ALU = mybir.AluOpType
+ACT = mybir.ActivationFunctionType
+
+P = 128
+PACK = 4
+K = Q // GROUP
+PART_ROW = 16
+
+
+def tile_attend_withoutconcept_claimants_rowchanges_pl_kernel(
+    tc, query, keys_words, keys_scales, concepts, part, lam, sres, slot_factor, vals, memq, offs, offs2,
+    out_0, out_1, out_2,
+):
+    nc = tc.nc
+    with ExitStack() as ctx:
+        sb = ctx.enter_context(tc.tile_pool(name="sb", bufs=1))
+        psum = ctx.enter_context(tc.psum_pool(name="psum", bufs=1))
+
+        def quantise(name, grouped, width):
+            codes = sb.tile([P, width], U32, name=name + "_codes", align_bytes=64)
+            scales = sb.tile([P, width], U8, name=name + "_scales", align_bytes=64)
+            nc.vector.quantize_mx(out=codes[:].bitcast(FP8X4), scales=scales[:], in_=grouped)
+            return codes, scales
+
+        part_pool = sb.tile([P, T], F32, name="part_pool")
+        nc.vector.memset(part_pool[:], 0.0)
+        key_scale_pool = sb.tile([P, T], U8, name="key_scale_pool")
+        nc.gpsimd.memset(key_scale_pool[:].bitcast(I32), 0)
+        ident = sb.tile([P, P], F32, name="ident")
+        make_identity(nc, ident[:])
+        shifted = sb.tile([P, PACK, Q], F32, name="shifted")
+        nc.vector.memset(shifted[:, :, 0:1], 0.0)
+
+        def load(name, shape, dtype, source):
+            tile = sb.tile(shape, dtype, name=name, align_bytes=64)
+            nc.sync.dma_start(tile[:], source)
+            return tile
+
+        def load_concepts(j):
+            return load("concept_pool%d" % j, [P, U], F32, concepts.rearrange("(p j) u -> j p u", j=PACK)[j])
+
+        def load_values(t):
+            return load("value_pool%d" % t, [P, T], F32, vals.rearrange("(p t) n -> t p n", t=PACK)[t])
+
+        tokens = load("tokens", [P, I // 16], U16, offs)
+        picks = load("picks", [P, I // 16], U16, offs2)
+        key_pool = sb.tile([P, T], U16, name="key_pool")
+        nc.sync.dma_start(key_pool[:].bitcast(I32), keys_words[0].bitcast(I32))
+        for quad in range(4):
+            nc.sync.dma_start(
+                key_scale_pool[32 * quad : 32 * quad + 4, :].bitcast(I32),
+                keys_scales[0][4 * quad : 4 * quad + 4, :].bitcast(I32),
+            )
+        query_raw = load("query_raw", [P, PACK, Q], F32, query.rearrange("(p j) q -> p j q", j=PACK))
+        concept_pool = [load_concepts(0), load_concepts(1)]
+        nc.sync.dma_start(part_pool[PART_ROW : PART_ROW + 1, :], part[0:1, :])
+        lam_cols = load("lam_cols", [P, 2], F32, lam.rearrange("(p c) o -> p (c o)", c=2))
+        memq_cols = load("memq_cols", [P, 2], F32, memq.rearrange("o (p c) -> p (o c)", c=2))
+        concept_pool.append(load_concepts(2))
+        concept_pool.append(load_concepts(3))
+        value_pool = [load_values(0)]
+        reserve = load("reserve", [P, PACK], F32, sres.rearrange("(p t) o -> p (t o)", t=PACK))
+        factor = load("factor", [P, PACK], F32, slot_factor.rearrange("o (p t) -> p (o t)", t=PACK))
+        for t in range(1, PACK):
+            value_pool.append(load_values(t))
+
+        key_listed = sb.tile([P, I], U16, name="key_listed")
+        nc.vector.tensor_copy(key_listed[:], key_pool[:].indirect(tokens[:]))
+        key_scales = sb.tile([P, I], U8, name="key_scales", align_bytes=64)
+        nc.vector.tensor_copy(
+            key_scales[:].rearrange("p (t m) -> p m t", t=PACK), key_scale_pool[:].indirect(tokens[:])
+        )
+        key_words = sb.tile([P, I], U16, name="key_words", align_bytes=64)
+        nc.vector.tensor_copy(
+            key_words[:].rearrange("p (t m) -> p t m", t=PACK), key_listed[:].rearrange("p (m t) -> p t m", t=PACK)
+        )
+
+        query_grouped = sb.tile([P, Q, PACK], BF16, name="query_grouped", align_bytes=64)
+        nc.scalar.copy(query_grouped[:], query_raw[:].rearrange("p j q -> p q j"))
+        q_codes, q_scales = quantise("query", query_grouped[:].rearrange("p q j -> p (q j)"), Q)
+
+        part_row = sb.tile([P, I], F32, name="part_row")
+        nc.vector.tensor_copy(part_row[:], part_pool[:].indirect(tokens[:]))
+
+        concept_listed = sb.tile([P, PACK, I], BF16, name="concept_listed")
+        nc.scalar.activation(concept_listed[:, 0, :], concept_pool[0][:].indirect(picks[:]), ACT.Copy)
+        nc.scalar.activation(concept_listed[:, 1, :], concept_pool[1][:].indirect(picks[:]), ACT.Copy)
+        nc.vector.tensor_copy(concept_listed[:, 2, :], concept_pool[2][:].indirect(picks[:]))
+        nc.scalar.activation(concept_listed[:, 3, 0 : I // 2], concept_pool[3][:].indirect(picks[:, 0:16]), ACT.Copy)
+        nc.vector.tensor_copy(concept_listed[:, 3, I // 2 : I], concept_pool[3][:].indirect(picks[:, 16:32]))
+
+        key_scores = sb.tile([P, PACK, Q], F32, name="key_scores", tag="concept_pool1", align_bytes=64)
+        for half in range(2):
+            bank = psum.tile([P, 2, Q], F32, name="key_bank", tag="bank%d" % half)
+            for r in range(2):
+                cols = slice((2 * half + r) * P, (2 * half + r + 1) * P)
+                nc.tensor.matmul_mx(
+                    out=bank[:, r, :], lhsT=key_words[:, cols].bitcast(FP4X4), lhsT_scale=key_scales[:, cols],
+                    rhs=q_codes[:].bitcast(FP8X4), rhs_scale=q_scales[:], start=True, stop=True,
+                )
+            nc.scalar.copy(key_scores[:, 2 * half : 2 * half + 2, :], bank[:])
+
+        part_turned = psum.tile([P, PACK, P], F32, name="part_turned", tag="bank4")
+        for t in range(PACK):
+            nc.tensor.transpose(part_turned[:, t, :], part_row[:, t::PACK], ident[:])
+        neg_part = sb.tile([P, PACK], F32, name="neg_part")
+        nc.scalar.activation(neg_part[:], part_turned[:, :, PART_ROW], ACT.Copy, scale=-1.0)
+
+        rows_turned = psum.tile([P, 2, 2, P], F32, name="rows_turned", tag="bank5")
+        for v, cols_tile in enumerate((lam_cols, memq_cols)):
+            for c in range(2):
+                nc.tensor.transpose(rows_turned[:, v, c, :], cols_tile[:, c : c + 1].to_broadcast([P, P]), ident[:])
+
+        def gather_values(t):
+            listed = sb.tile([P, I], BF16, name="value_listed%d" % t)
+            nc.scalar.activation(listed[:], value_pool[t][:].indirect(tokens[:]), ACT.Copy)
+            words = listed[:].bitcast(F32)
+            turned = psum.tile([P, 2, P], F32, name="value_turned", tag="bank%d" % (4 + t))
+            for u in range(2):
+                nc.tensor.transpose(turned[:, u, :], words[:, u::2], ident[:])
+            return turned
+
+        def quantise_values(t, turned, tag):
+            v_grouped = sb.tile([P, P * PACK], BF16, name="value_grouped%d" % t, tag=tag, align_bytes=64)
+            nc.scalar.copy(v_grouped[:].bitcast(F32).rearrange("p (e u) -> p e u", u=2), turned[:].rearrange("p u e -> p e u"))
+            return quantise("value%d" % t, v_grouped[:], P)
+
+        values = [quantise_values(0, gather_values(0), "value_grouped0")]
+
+        scores = sb.tile([P, PACK, Q], F32, name="scores")
+        scaled = sb.tile([P, PACK, Q], F32, name="scaled")
+        weights = sb.tile([P, PACK, Q], F32, name="weights", tag="value_pool0", align_bytes=64)
+        sums = sb.tile([P, PACK, K], F32, name="sums")
+        denominators = sb.tile([P, PACK, K], F32, name="denominators")
+        inverses = sb.tile([P, PACK, K], F32, name="inverses")
+        gains = sb.tile([P, K, PACK], F32, name="gains")
+        dealt = concept_listed[:].rearrange("p j (m t) -> p t m j", t=PACK)
+        banks = []
+        for half in range(2):
+            bank = psum.tile([P, 2, Q], F32, name="concept_bank", tag="bank%d" % (2 + half))
+            banks.append(bank)
+            for r in range(2):
+                t = 2 * half + r
+                c_grouped = sb.tile([P, P, PACK], BF16, name="concept_grouped%d" % t, align_bytes=64)
+                if half == 0:
+                    nc.vector.tensor_copy(c_grouped[:], dealt[:, t])
+                else:
+                    nc.scalar.copy(c_grouped[:], dealt[:, t])
+                c_codes, c_scales = quantise("concept%d" % t, c_grouped[:].rearrange("p m j -> p (m j)"), P)
+                nc.tensor.matmul_mx(
+                    out=bank[:, r, :], lhsT=c_codes[:].bitcast(FP8X4), lhsT_scale=c_scales[:],
+                    rhs=q_codes[:].bitcast(FP8X4), rhs_scale=q_scales[:], start=True, stop=True,
+                )
+        rows = sb.tile([P, 2, Q], F32, name="rows", tag="concept_pool3", align_bytes=64)
+        nc.scalar.copy(rows[:].rearrange("p v (n c) -> p v n c", c=2), rows_turned[:].rearrange("p v c n -> p v n c"))
+        for half in range(2):
+            pair = slice(2 * half, 2 * half + 2)
+            for r in range(2):
+                t = 2 * half + r
+                nc.vector.scalar_tensor_tensor(
+                    scores[:, t, :], banks[half][:, r, :], neg_part[:, t : t + 1], key_scores[:, t, :], ALU.mult, ALU.add
+                )
+            nc.vector.tensor_tensor(scaled[:, pair, :], scores[:, pair, :], rows[:, 0:1, :].to_broadcast([P, 2, Q]), ALU.mult)
+            nc.scalar.activation(weights[:, pair, :], scaled[:, pair, :], ACT.Exp)
+        for half in range(2):
+            pair = slice(2 * half, 2 * half + 2)
+            nc.vector.tensor_reduce(
+                sums[:, pair, :], weights[:, pair, :].rearrange("p t (k j) -> p t k j", j=GROUP), mybir.AxisListType.X, ALU.add
+            )
+            nc.vector.tensor_tensor(
+                denominators[:, pair, :], sums[:, pair, :], reserve[:, pair].unsqueeze(2).to_broadcast([P, 2, K]), ALU.add
+            )
+            nc.vector.reciprocal(inverses[:, pair, :], denominators[:, pair, :])
+        nc.vector.tensor_tensor(
+            gains[:], inverses[:].rearrange("p t k -> p k t"), factor[:].unsqueeze(1).to_broadcast([P, K, PACK]), ALU.mult
+        )
+        weight_grouped = sb.tile([P, Q, PACK], BF16, name="weight_grouped", align_bytes=64)
+        nc.vector.tensor_tensor(
+            weight_grouped[:].rearrange("p (k j) t -> p k j t", j=GROUP),
+            weights[:].rearrange("p t (k j) -> p k j t", j=GROUP),
+            gains[:].unsqueeze(2).to_broadcast([P, K, GROUP, PACK]),
+            ALU.mult,
+        )
+        w_codes, w_scales = quantise("weight", weight_grouped[:].rearrange("p q t -> p (q t)"), Q)
+
+        turned = [gather_values(t) for t in range(1, PACK)]
+        values.append(quantise_values(1, turned[0], "value_pool2"))
+        values.append(quantise_values(2, turned[1], "value_pool3"))
+        values.append(quantise_values(3, turned[2], "value_grouped3"))
+        result = sb.tile([P, PACK, Q], F32, name="result")
+        for t in range(PACK):
+            v_codes, v_scales = values[t]
+            bank = psum.tile([P, Q], F32, name="result_bank", tag="bank%d" % (5, 7, 0, 1)[t])
+            nc.tensor.matmul_mx(
+                out=bank[:], lhsT=v_codes[:].bitcast(FP8X4), lhsT_scale=v_scales[:],
+                rhs=w_codes[:].bitcast(FP8X4), rhs_scale=w_scales[:], start=True, stop=True,
+            )
+            nc.vector.tensor_tensor(shifted[:, t, 1:Q], bank[:, 0 : Q - 1], rows[:, 1, 1:Q], ALU.mult)
+            nc.vector.tensor_tensor(result[:, t, :], bank[:], shifted[:, t, :], ALU.subtract)
+            nc.sync.dma_start(out_0.rearrange("(p t) q -> t p q", t=PACK)[t], result[:, t, :])
+
+        result_grouped = sb.tile([P, Q, PACK], BF16, name="result_grouped", align_bytes=64)
+        nc.vector.tensor_copy(result_grouped[:], result[:].rearrange("p t q -> p q t"))
+        y_codes, y_scales = quantise("result", result_grouped[:].rearrange("p q t -> p (q t)"), Q)
+        nc.sync.dma_start(out_1[0].rearrange("p c r -> p (c r)").bitcast(I32), y_codes[:].bitcast(I32))
+        for quad in range(4):
+            queue = nc.scalar if quad % 2 == 0 else nc.sync
+            queue.dma_start(
+                out_2[0][4 * quad : 4 * quad + 4, :].bitcast(I32), y_scales[32 * quad : 32 * quad + 4, :].bitcast(I32)
+            )

@@ -21,6 +21,8 @@ P = 128
 PACK = 4
 K = Q // GROUP
 PART_ROW = 16
+RUN = 4
+CAST_SPLIT = 160
 
 
 def tile_attend_withoutconcept_claimants_rowchanges_pl_kernel(
@@ -32,8 +34,8 @@ def tile_attend_withoutconcept_claimants_rowchanges_pl_kernel(
         sb = ctx.enter_context(tc.tile_pool(name="sb", bufs=1))
         psum = ctx.enter_context(tc.psum_pool(name="psum", bufs=1))
 
-        def quantise(name, grouped, width):
-            codes = sb.tile([P, width], U32, name=name + "_codes", align_bytes=64)
+        def quantise(name, grouped, width, codes_tag=""):
+            codes = sb.tile([P, width], U32, name=name + "_codes", tag=codes_tag, align_bytes=64)
             scales = sb.tile([P, width], U8, name=name + "_scales", align_bytes=64)
             nc.vector.quantize_mx(out=codes[:].bitcast(FP8X4), scales=scales[:], in_=grouped)
             return codes, scales
@@ -45,7 +47,7 @@ def tile_attend_withoutconcept_claimants_rowchanges_pl_kernel(
         ident = sb.tile([P, P], F32, name="ident")
         make_identity(nc, ident[:])
         shifted = sb.tile([P, PACK, Q], F32, name="shifted")
-        nc.vector.memset(shifted[:, :, 0:1], 0.0)
+        nc.scalar.activation(shifted[:, :, 0], ident[:, 0:PACK], ACT.Copy, scale=0.0)
 
         def load(name, shape, dtype, source):
             tile = sb.tile(shape, dtype, name=name, align_bytes=64)
@@ -60,43 +62,51 @@ def tile_attend_withoutconcept_claimants_rowchanges_pl_kernel(
 
         tokens = load("tokens", [P, I // 16], U16, offs)
         picks = load("picks", [P, I // 16], U16, offs2)
+        lam_cols = load("lam_cols", [P, 2], F32, lam.rearrange("(p c) o -> p (c o)", c=2))
+        memq_cols = load("memq_cols", [P, 2], F32, memq.rearrange("o (p c) -> p (o c)", c=2))
         key_pool = sb.tile([P, T], U16, name="key_pool")
         nc.sync.dma_start(key_pool[:].bitcast(I32), keys_words[0].bitcast(I32))
+        query_raw = load("query_raw", [P, PACK, Q], F32, query.rearrange("(p j) q -> p j q", j=PACK))
+        nc.sync.dma_start(part_pool[PART_ROW : PART_ROW + 1, :], part[0:1, :])
         for quad in range(4):
             nc.sync.dma_start(
                 key_scale_pool[32 * quad : 32 * quad + 4, :].bitcast(I32),
                 keys_scales[0][4 * quad : 4 * quad + 4, :].bitcast(I32),
             )
-        query_raw = load("query_raw", [P, PACK, Q], F32, query.rearrange("(p j) q -> p j q", j=PACK))
-        concept_pool = [load_concepts(0), load_concepts(1)]
-        nc.sync.dma_start(part_pool[PART_ROW : PART_ROW + 1, :], part[0:1, :])
-        lam_cols = load("lam_cols", [P, 2], F32, lam.rearrange("(p c) o -> p (c o)", c=2))
-        memq_cols = load("memq_cols", [P, 2], F32, memq.rearrange("o (p c) -> p (o c)", c=2))
-        concept_pool.append(load_concepts(2))
-        concept_pool.append(load_concepts(3))
+        concept_pool = [load_concepts(j) for j in range(PACK)]
         value_pool = [load_values(0)]
         reserve = load("reserve", [P, PACK], F32, sres.rearrange("(p t) o -> p (t o)", t=PACK))
         factor = load("factor", [P, PACK], F32, slot_factor.rearrange("o (p t) -> p (o t)", t=PACK))
         for t in range(1, PACK):
             value_pool.append(load_values(t))
 
+        rows_turned = psum.tile([P, 2, 2, P], F32, name="rows_turned", tag="bank5")
+        for v, cols_tile in enumerate((lam_cols, memq_cols)):
+            for c in range(2):
+                nc.tensor.transpose(rows_turned[:, v, c, :], cols_tile[:, c : c + 1].to_broadcast([P, P]), ident[:])
+        rows = sb.tile([P, 2, Q], F32, name="rows")
+        nc.scalar.activation(
+            rows[:].rearrange("p v (n c) -> p v n c", c=2), rows_turned[:].rearrange("p v c n -> p v n c"), ACT.Copy
+        )
+
         key_listed = sb.tile([P, I], U16, name="key_listed")
         nc.vector.tensor_copy(key_listed[:], key_pool[:].indirect(tokens[:]))
+        query_grouped = sb.tile([P, Q, PACK], BF16, name="query_grouped", align_bytes=64)
+        nc.vector.tensor_copy(
+            query_grouped[:].rearrange("p (c i) j -> p c j i", i=RUN), query_raw[:].rearrange("p j (c i) -> p c j i", i=RUN)
+        )
         key_scales = sb.tile([P, I], U8, name="key_scales", align_bytes=64)
         nc.vector.tensor_copy(
             key_scales[:].rearrange("p (t m) -> p m t", t=PACK), key_scale_pool[:].indirect(tokens[:])
         )
         key_words = sb.tile([P, I], U16, name="key_words", align_bytes=64)
         nc.vector.tensor_copy(
-            key_words[:].rearrange("p (t m) -> p t m", t=PACK), key_listed[:].rearrange("p (m t) -> p t m", t=PACK)
+            key_words[:].rearrange("p (t m) -> p m t", t=PACK), key_listed[:].rearrange("p (m t) -> p m t", t=PACK)
         )
-
-        query_grouped = sb.tile([P, Q, PACK], BF16, name="query_grouped", align_bytes=64)
-        nc.scalar.copy(query_grouped[:], query_raw[:].rearrange("p j q -> p q j"))
         q_codes, q_scales = quantise("query", query_grouped[:].rearrange("p q j -> p (q j)"), Q)
 
         part_row = sb.tile([P, I], F32, name="part_row")
-        nc.vector.tensor_copy(part_row[:], part_pool[:].indirect(tokens[:]))
+        nc.scalar.activation(part_row[:], part_pool[:].indirect(tokens[:]), ACT.Copy)
 
         concept_listed = sb.tile([P, PACK, I], BF16, name="concept_listed")
         nc.scalar.activation(concept_listed[:, 0, :], concept_pool[0][:].indirect(picks[:]), ACT.Copy)
@@ -105,27 +115,41 @@ def tile_attend_withoutconcept_claimants_rowchanges_pl_kernel(
         nc.scalar.activation(concept_listed[:, 3, 0 : I // 2], concept_pool[3][:].indirect(picks[:, 0:16]), ACT.Copy)
         nc.vector.tensor_copy(concept_listed[:, 3, I // 2 : I], concept_pool[3][:].indirect(picks[:, 16:32]))
 
-        key_scores = sb.tile([P, PACK, Q], F32, name="key_scores", tag="concept_pool1", align_bytes=64)
-        for half in range(2):
-            bank = psum.tile([P, 2, Q], F32, name="key_bank", tag="bank%d" % half)
-            for r in range(2):
-                cols = slice((2 * half + r) * P, (2 * half + r + 1) * P)
-                nc.tensor.matmul_mx(
-                    out=bank[:, r, :], lhsT=key_words[:, cols].bitcast(FP4X4), lhsT_scale=key_scales[:, cols],
-                    rhs=q_codes[:].bitcast(FP8X4), rhs_scale=q_scales[:], start=True, stop=True,
-                )
-            nc.scalar.copy(key_scores[:, 2 * half : 2 * half + 2, :], bank[:])
-
         part_turned = psum.tile([P, PACK, P], F32, name="part_turned", tag="bank4")
         for t in range(PACK):
             nc.tensor.transpose(part_turned[:, t, :], part_row[:, t::PACK], ident[:])
-        neg_part = sb.tile([P, PACK], F32, name="neg_part")
+        neg_part = sb.tile([P, PACK], F32, name="neg_part", tag="concept_pool0", align_bytes=64)
         nc.scalar.activation(neg_part[:], part_turned[:, :, PART_ROW], ACT.Copy, scale=-1.0)
 
-        rows_turned = psum.tile([P, 2, 2, P], F32, name="rows_turned", tag="bank5")
-        for v, cols_tile in enumerate((lam_cols, memq_cols)):
-            for c in range(2):
-                nc.tensor.transpose(rows_turned[:, v, c, :], cols_tile[:, c : c + 1].to_broadcast([P, P]), ident[:])
+        def score_bank(tag, codes, scales):
+            bank = psum.tile([P, 2, Q], F32, name="score_bank", tag=tag)
+            for r in range(2):
+                cols = slice(r * P, (r + 1) * P)
+                nc.tensor.matmul_mx(
+                    out=bank[:, r, :], lhsT=codes[:, cols], lhsT_scale=scales[:, cols],
+                    rhs=q_codes[:].bitcast(FP8X4), rhs_scale=q_scales[:], start=True, stop=True,
+                )
+            return bank
+
+        key_banks = []
+        for half in range(2):
+            cols = slice(2 * half * P, (2 * half + 2) * P)
+            key_banks.append(score_bank("bank%d" % half, key_words[:, cols].bitcast(FP4X4), key_scales[:, cols]))
+
+        concept_banks = []
+        dealt = concept_listed[:].rearrange("p j (a i t) -> p a j i t", i=2, t=PACK)
+        for half in range(2):
+            c_grouped = sb.tile([P, 2, P, PACK], BF16, name="concept_grouped%d" % half, align_bytes=64)
+            copy = nc.vector.tensor_copy if half == 0 else nc.scalar.copy
+            copy(c_grouped[:].rearrange("p t (a i) j -> p a j i t", i=2), dealt[:, :, :, :, 2 * half : 2 * half + 2])
+            c_codes, c_scales = quantise("concept%d" % half, c_grouped[:].rearrange("p t m j -> p (t m j)"), 2 * P)
+            concept_banks.append(score_bank("bank%d" % (2 + half), c_codes[:].bitcast(FP8X4), c_scales[:]))
+
+        key_scores = []
+        for half, (copy, tag) in enumerate(((nc.scalar.copy, "concept_pool3"), (nc.vector.tensor_copy, "concept_grouped1"))):
+            pair_scores = sb.tile([P, 2, Q], F32, name="key_scores%d" % half, tag=tag, align_bytes=64)
+            copy(pair_scores[:], key_banks[half][:])
+            key_scores.append(pair_scores)
 
         def gather_values(t):
             listed = sb.tile([P, I], BF16, name="value_listed%d" % t)
@@ -141,43 +165,26 @@ def tile_attend_withoutconcept_claimants_rowchanges_pl_kernel(
             nc.scalar.copy(v_grouped[:].bitcast(F32).rearrange("p (e u) -> p e u", u=2), turned[:].rearrange("p u e -> p e u"))
             return quantise("value%d" % t, v_grouped[:], P)
 
-        values = [quantise_values(0, gather_values(0), "value_grouped0")]
+        turned = [gather_values(0), gather_values(1)]
 
         scores = sb.tile([P, PACK, Q], F32, name="scores")
-        scaled = sb.tile([P, PACK, Q], F32, name="scaled")
-        weights = sb.tile([P, PACK, Q], F32, name="weights", tag="value_pool0", align_bytes=64)
-        sums = sb.tile([P, PACK, K], F32, name="sums")
-        denominators = sb.tile([P, PACK, K], F32, name="denominators")
-        inverses = sb.tile([P, PACK, K], F32, name="inverses")
-        gains = sb.tile([P, K, PACK], F32, name="gains")
-        dealt = concept_listed[:].rearrange("p j (m t) -> p t m j", t=PACK)
-        banks = []
-        for half in range(2):
-            bank = psum.tile([P, 2, Q], F32, name="concept_bank", tag="bank%d" % (2 + half))
-            banks.append(bank)
-            for r in range(2):
-                t = 2 * half + r
-                c_grouped = sb.tile([P, P, PACK], BF16, name="concept_grouped%d" % t, align_bytes=64)
-                if half == 0:
-                    nc.vector.tensor_copy(c_grouped[:], dealt[:, t])
-                else:
-                    nc.scalar.copy(c_grouped[:], dealt[:, t])
-                c_codes, c_scales = quantise("concept%d" % t, c_grouped[:].rearrange("p m j -> p (m j)"), P)
-                nc.tensor.matmul_mx(
-                    out=bank[:, r, :], lhsT=c_codes[:].bitcast(FP8X4), lhsT_scale=c_scales[:],
-                    rhs=q_codes[:].bitcast(FP8X4), rhs_scale=q_scales[:], start=True, stop=True,
-                )
-        rows = sb.tile([P, 2, Q], F32, name="rows", tag="concept_pool3", align_bytes=64)
-        nc.scalar.copy(rows[:].rearrange("p v (n c) -> p v n c", c=2), rows_turned[:].rearrange("p v c n -> p v n c"))
+        scaled = sb.tile([P, PACK, Q], F32, name="scaled", align_bytes=64)
+        weights = sb.tile([P, PACK, Q], F32, name="weights", tag="value_pool1", align_bytes=64)
         for half in range(2):
             pair = slice(2 * half, 2 * half + 2)
             for r in range(2):
                 t = 2 * half + r
                 nc.vector.scalar_tensor_tensor(
-                    scores[:, t, :], banks[half][:, r, :], neg_part[:, t : t + 1], key_scores[:, t, :], ALU.mult, ALU.add
+                    scores[:, t, :], concept_banks[half][:, r, :], neg_part[:, t : t + 1], key_scores[half][:, r, :],
+                    ALU.mult, ALU.add,
                 )
             nc.vector.tensor_tensor(scaled[:, pair, :], scores[:, pair, :], rows[:, 0:1, :].to_broadcast([P, 2, Q]), ALU.mult)
             nc.scalar.activation(weights[:, pair, :], scaled[:, pair, :], ACT.Exp)
+        values = [quantise_values(0, turned[0], "scaled")]
+
+        sums = sb.tile([P, PACK, K], F32, name="sums")
+        denominators = sb.tile([P, PACK, K], F32, name="denominators")
+        inverses = sb.tile([P, PACK, K], F32, name="inverses")
         for half in range(2):
             pair = slice(2 * half, 2 * half + 2)
             nc.vector.tensor_reduce(
@@ -187,26 +194,33 @@ def tile_attend_withoutconcept_claimants_rowchanges_pl_kernel(
                 denominators[:, pair, :], sums[:, pair, :], reserve[:, pair].unsqueeze(2).to_broadcast([P, 2, K]), ALU.add
             )
             nc.vector.reciprocal(inverses[:, pair, :], denominators[:, pair, :])
+        runs = GROUP // RUN
+        gains = sb.tile([P, K, runs, PACK], F32, name="gains")
         nc.vector.tensor_tensor(
-            gains[:], inverses[:].rearrange("p t k -> p k t"), factor[:].unsqueeze(1).to_broadcast([P, K, PACK]), ALU.mult
+            gains[:],
+            inverses[:].rearrange("p t k -> p k t").unsqueeze(2).to_broadcast([P, K, runs, PACK]),
+            factor[:].unsqueeze(1).unsqueeze(1).to_broadcast([P, K, runs, PACK]),
+            ALU.mult,
         )
         weight_grouped = sb.tile([P, Q, PACK], BF16, name="weight_grouped", align_bytes=64)
         nc.vector.tensor_tensor(
-            weight_grouped[:].rearrange("p (k j) t -> p k j t", j=GROUP),
-            weights[:].rearrange("p t (k j) -> p k j t", j=GROUP),
-            gains[:].unsqueeze(2).to_broadcast([P, K, GROUP, PACK]),
+            weight_grouped[:].rearrange("p (c i) t -> p c t i", i=RUN),
+            weights[:].rearrange("p t (c i) -> p c t i", i=RUN),
+            gains[:].rearrange("p k h t -> p (k h) t").unsqueeze(3).to_broadcast([P, Q // RUN, PACK, RUN]),
             ALU.mult,
         )
-        w_codes, w_scales = quantise("weight", weight_grouped[:].rearrange("p q t -> p (q t)"), Q)
 
-        turned = [gather_values(t) for t in range(1, PACK)]
-        values.append(quantise_values(1, turned[0], "value_pool2"))
-        values.append(quantise_values(2, turned[1], "value_pool3"))
-        values.append(quantise_values(3, turned[2], "value_grouped3"))
+        turned += [gather_values(2), gather_values(3)]
+        values.append(quantise_values(1, turned[1], "value_pool2"))
+        values.append(quantise_values(2, turned[2], "value_pool3"))
+        values.append(quantise_values(3, turned[3], "value_grouped3"))
+        w_codes, w_scales = quantise(
+            "weight", weight_grouped[:].rearrange("p q t -> p (q t)"), Q, codes_tag="value_pool3"
+        )
         result = sb.tile([P, PACK, Q], F32, name="result")
         for t in range(PACK):
             v_codes, v_scales = values[t]
-            bank = psum.tile([P, Q], F32, name="result_bank", tag="bank%d" % (5, 7, 0, 1)[t])
+            bank = psum.tile([P, Q], F32, name="result_bank", tag="bank%d" % t)
             nc.tensor.matmul_mx(
                 out=bank[:], lhsT=v_codes[:].bitcast(FP8X4), lhsT_scale=v_scales[:],
                 rhs=w_codes[:].bitcast(FP8X4), rhs_scale=w_scales[:], start=True, stop=True,
@@ -216,7 +230,11 @@ def tile_attend_withoutconcept_claimants_rowchanges_pl_kernel(
             nc.sync.dma_start(out_0.rearrange("(p t) q -> t p q", t=PACK)[t], result[:, t, :])
 
         result_grouped = sb.tile([P, Q, PACK], BF16, name="result_grouped", align_bytes=64)
-        nc.vector.tensor_copy(result_grouped[:], result[:].rearrange("p t q -> p q t"))
+        for copy, cols in ((nc.vector.tensor_copy, slice(0, CAST_SPLIT)), (nc.scalar.copy, slice(CAST_SPLIT, Q))):
+            copy(
+                result_grouped[:, cols, :].rearrange("p (c i) t -> p c t i", i=RUN),
+                result[:, :, cols].rearrange("p t (c i) -> p c t i", i=RUN),
+            )
         y_codes, y_scales = quantise("result", result_grouped[:].rearrange("p q t -> p (q t)"), Q)
         nc.sync.dma_start(out_1[0].rearrange("p c r -> p (c r)").bitcast(I32), y_codes[:].bitcast(I32))
         for quad in range(4):

@@ -40,33 +40,37 @@ def tile_attend_withoutconcept_claimants_rowchanges_pl_kernel(
             nc.vector.quantize_mx(out=codes[:].bitcast(FP8X4), scales=scales[:], in_=grouped)
             return codes, scales
 
+        ident = sb.tile([P, P], F32, name="ident")
+        nc.vector.memset(ident[:], 0.0)
         part_pool = sb.tile([P, T], F32, name="part_pool")
         nc.vector.memset(part_pool[:], 0.0)
         key_scale_pool = sb.tile([P, T], U8, name="key_scale_pool")
         nc.gpsimd.memset(key_scale_pool[:].bitcast(I32), 0)
-        ident = sb.tile([P, P], F32, name="ident")
-        make_identity(nc, ident[:])
+        make_identity(nc, ident[:], nomemset=True)
         shifted = sb.tile([P, PACK, Q], F32, name="shifted")
         nc.scalar.activation(shifted[:, :, 0], ident[:, 0:PACK], ACT.Copy, scale=0.0)
 
-        def load(name, shape, dtype, source):
+        def load(queue, name, shape, dtype, source):
             tile = sb.tile(shape, dtype, name=name, align_bytes=64)
-            nc.sync.dma_start(tile[:], source)
+            queue.dma_start(tile[:], source)
             return tile
 
         def load_concepts(j):
-            return load("concept_pool%d" % j, [P, U], F32, concepts.rearrange("(p j) u -> j p u", j=PACK)[j])
+            return load(nc.sync, "concept_pool%d" % j, [P, U], F32, concepts.rearrange("(p j) u -> j p u", j=PACK)[j])
 
         def load_values(t):
-            return load("value_pool%d" % t, [P, T], F32, vals.rearrange("(p t) n -> t p n", t=PACK)[t])
+            return load(nc.sync, "value_pool%d" % t, [P, T], F32, vals.rearrange("(p t) n -> t p n", t=PACK)[t])
 
-        tokens = load("tokens", [P, I // 16], U16, offs)
-        picks = load("picks", [P, I // 16], U16, offs2)
-        lam_cols = load("lam_cols", [P, 2], F32, lam.rearrange("(p c) o -> p (c o)", c=2))
-        memq_cols = load("memq_cols", [P, 2], F32, memq.rearrange("o (p c) -> p (o c)", c=2))
+        reserve = load(nc.gpsimd, "reserve", [P, PACK], F32, sres.rearrange("(p t) o -> p (t o)", t=PACK))
+        factor = load(nc.gpsimd, "factor", [P, PACK], F32, slot_factor.rearrange("o (p t) -> p (o t)", t=PACK))
+
+        tokens = load(nc.sync, "tokens", [P, I // 16], U16, offs)
+        picks = load(nc.sync, "picks", [P, I // 16], U16, offs2)
+        lam_cols = load(nc.sync, "lam_cols", [P, 2], F32, lam.rearrange("(p c) o -> p (c o)", c=2))
+        memq_cols = load(nc.sync, "memq_cols", [P, 2], F32, memq.rearrange("o (p c) -> p (o c)", c=2))
         key_pool = sb.tile([P, T], U16, name="key_pool")
         nc.sync.dma_start(key_pool[:].bitcast(I32), keys_words[0].bitcast(I32))
-        query_raw = load("query_raw", [P, PACK, Q], F32, query.rearrange("(p j) q -> p j q", j=PACK))
+        query_raw = load(nc.sync, "query_raw", [P, PACK, Q], F32, query.rearrange("(p j) q -> p j q", j=PACK))
         nc.sync.dma_start(part_pool[PART_ROW : PART_ROW + 1, :], part[0:1, :])
         for quad in range(4):
             nc.sync.dma_start(
@@ -74,11 +78,7 @@ def tile_attend_withoutconcept_claimants_rowchanges_pl_kernel(
                 keys_scales[0][4 * quad : 4 * quad + 4, :].bitcast(I32),
             )
         concept_pool = [load_concepts(j) for j in range(PACK)]
-        value_pool = [load_values(0)]
-        reserve = load("reserve", [P, PACK], F32, sres.rearrange("(p t) o -> p (t o)", t=PACK))
-        factor = load("factor", [P, PACK], F32, slot_factor.rearrange("o (p t) -> p (o t)", t=PACK))
-        for t in range(1, PACK):
-            value_pool.append(load_values(t))
+        value_pool = [load_values(t) for t in range(PACK)]
 
         rows_turned = psum.tile([P, 2, 2, P], F32, name="rows_turned", tag="bank5")
         for v, cols_tile in enumerate((lam_cols, memq_cols)):
@@ -151,6 +151,9 @@ def tile_attend_withoutconcept_claimants_rowchanges_pl_kernel(
             copy(pair_scores[:], key_banks[half][:])
             key_scores.append(pair_scores)
 
+        inverse_factor = sb.tile([P, PACK], F32, name="inverse_factor", tag="concept_grouped0", align_bytes=64)
+        nc.vector.reciprocal(inverse_factor[:], factor[:])
+
         def gather_values(t):
             listed = sb.tile([P, I], BF16, name="value_listed%d" % t)
             nc.scalar.activation(listed[:], value_pool[t][:].indirect(tokens[:]), ACT.Copy)
@@ -160,15 +163,13 @@ def tile_attend_withoutconcept_claimants_rowchanges_pl_kernel(
                 nc.tensor.transpose(turned[:, u, :], words[:, u::2], ident[:])
             return turned
 
-        def quantise_values(t, turned, tag):
-            v_grouped = sb.tile([P, P * PACK], BF16, name="value_grouped%d" % t, tag=tag, align_bytes=64)
-            nc.scalar.copy(v_grouped[:].bitcast(F32).rearrange("p (e u) -> p e u", u=2), turned[:].rearrange("p u e -> p e u"))
-            return quantise("value%d" % t, v_grouped[:], P)
+        def quantise_values(t, turned, v_grouped):
+            nc.scalar.copy(v_grouped.bitcast(F32).rearrange("p (e u) -> p e u", u=2), turned[:].rearrange("p u e -> p e u"))
+            return quantise("value%d" % t, v_grouped, P)
 
         turned = [gather_values(0), gather_values(1)]
 
         scores = sb.tile([P, PACK, Q], F32, name="scores")
-        scaled = sb.tile([P, PACK, Q], F32, name="scaled", align_bytes=64)
         weights = sb.tile([P, PACK, Q], F32, name="weights", tag="value_pool1", align_bytes=64)
         for half in range(2):
             pair = slice(2 * half, 2 * half + 2)
@@ -178,45 +179,44 @@ def tile_attend_withoutconcept_claimants_rowchanges_pl_kernel(
                     scores[:, t, :], concept_banks[half][:, r, :], neg_part[:, t : t + 1], key_scores[half][:, r, :],
                     ALU.mult, ALU.add,
                 )
-            nc.vector.tensor_tensor(scaled[:, pair, :], scores[:, pair, :], rows[:, 0:1, :].to_broadcast([P, 2, Q]), ALU.mult)
-            nc.scalar.activation(weights[:, pair, :], scaled[:, pair, :], ACT.Exp)
-        values = [quantise_values(0, turned[0], "scaled")]
+            scaled = sb.tile([P, 2, Q], F32, name="scaled%d" % half, align_bytes=64)
+            nc.vector.tensor_tensor(scaled[:], scores[:, pair, :], rows[:, 0:1, :].to_broadcast([P, 2, Q]), ALU.mult)
+            nc.scalar.activation(weights[:, pair, :], scaled[:], ACT.Exp)
 
         sums = sb.tile([P, PACK, K], F32, name="sums")
-        denominators = sb.tile([P, PACK, K], F32, name="denominators")
-        inverses = sb.tile([P, PACK, K], F32, name="inverses")
+        denominators = sb.tile([P, K, PACK], F32, name="denominators")
+        gains = sb.tile([P, K, PACK], F32, name="gains")
         for half in range(2):
             pair = slice(2 * half, 2 * half + 2)
             nc.vector.tensor_reduce(
                 sums[:, pair, :], weights[:, pair, :].rearrange("p t (k j) -> p t k j", j=GROUP), mybir.AxisListType.X, ALU.add
             )
-            nc.vector.tensor_tensor(
-                denominators[:, pair, :], sums[:, pair, :], reserve[:, pair].unsqueeze(2).to_broadcast([P, 2, K]), ALU.add
-            )
-            nc.vector.reciprocal(inverses[:, pair, :], denominators[:, pair, :])
-        runs = GROUP // RUN
-        gains = sb.tile([P, K, runs, PACK], F32, name="gains")
-        nc.vector.tensor_tensor(
-            gains[:],
-            inverses[:].rearrange("p t k -> p k t").unsqueeze(2).to_broadcast([P, K, runs, PACK]),
-            factor[:].unsqueeze(1).unsqueeze(1).to_broadcast([P, K, runs, PACK]),
-            ALU.mult,
-        )
+            for t in (2 * half, 2 * half + 1):
+                nc.vector.tensor_scalar(
+                    denominators[:, :, t], sums[:, t, :], reserve[:, t : t + 1], inverse_factor[:, t : t + 1],
+                    ALU.add, ALU.mult,
+                )
+            nc.vector.reciprocal(gains[:, :, pair], denominators[:, :, pair])
         weight_grouped = sb.tile([P, Q, PACK], BF16, name="weight_grouped", align_bytes=64)
-        nc.vector.tensor_tensor(
-            weight_grouped[:].rearrange("p (c i) t -> p c t i", i=RUN),
-            weights[:].rearrange("p t (c i) -> p c t i", i=RUN),
-            gains[:].rearrange("p k h t -> p (k h) t").unsqueeze(3).to_broadcast([P, Q // RUN, PACK, RUN]),
-            ALU.mult,
-        )
+        for h in range(GROUP // RUN):
+            nc.vector.tensor_tensor(
+                weight_grouped[:].rearrange("p (k h i) t -> p h k t i", k=K, i=RUN)[:, h],
+                weights[:].rearrange("p t (k h i) -> p h k t i", k=K, i=RUN)[:, h],
+                gains[:].unsqueeze(3).to_broadcast([P, K, PACK, RUN]),
+                ALU.mult,
+            )
 
+        first_grouped = sb.tile([P, P * PACK], BF16, name="first_grouped", tag="scaled0", align_bytes=64)
+        values = [quantise_values(0, turned[0], first_grouped[:])]
         turned += [gather_values(2), gather_values(3)]
-        values.append(quantise_values(1, turned[1], "value_pool2"))
-        values.append(quantise_values(2, turned[2], "value_pool3"))
-        values.append(quantise_values(3, turned[3], "value_grouped3"))
+        second_grouped = sb.tile([P, P * PACK], BF16, name="second_grouped", tag="value_pool2", align_bytes=64)
+        third_grouped = sb.tile([P, P * PACK], BF16, name="third_grouped", align_bytes=64)
+        last_grouped = sb.tile([P, P * PACK], BF16, name="last_grouped", align_bytes=64)
+        values += [quantise_values(1, turned[1], second_grouped[:]), quantise_values(2, turned[2], third_grouped[:])]
         w_codes, w_scales = quantise(
             "weight", weight_grouped[:].rearrange("p q t -> p (q t)"), Q, codes_tag="value_pool3"
         )
+        values.append(quantise_values(3, turned[3], last_grouped[:]))
         result = sb.tile([P, PACK, Q], F32, name="result")
         for t in range(PACK):
             v_codes, v_scales = values[t]

@@ -23,6 +23,7 @@ K = Q // GROUP
 PART_ROW = 16
 RUN = 4
 CAST_SPLIT = 160
+LAST_SPLIT = 288
 
 
 def tile_attend_withoutconcept_claimants_rowchanges_pl_kernel(
@@ -32,10 +33,11 @@ def tile_attend_withoutconcept_claimants_rowchanges_pl_kernel(
     nc = tc.nc
     with ExitStack() as ctx:
         sb = ctx.enter_context(tc.tile_pool(name="sb", bufs=1))
+        last = ctx.enter_context(tc.tile_pool(name="last", bufs=1))
         psum = ctx.enter_context(tc.psum_pool(name="psum", bufs=1))
 
-        def quantise(name, grouped, width, codes_tag=""):
-            codes = sb.tile([P, width], U32, name=name + "_codes", tag=codes_tag, align_bytes=64)
+        def quantise(name, grouped, width):
+            codes = sb.tile([P, width], U32, name=name + "_codes", align_bytes=64)
             scales = sb.tile([P, width], U8, name=name + "_scales", align_bytes=64)
             nc.vector.quantize_mx(out=codes[:].bitcast(FP8X4), scales=scales[:], in_=grouped)
             return codes, scales
@@ -78,9 +80,12 @@ def tile_attend_withoutconcept_claimants_rowchanges_pl_kernel(
                 keys_scales[0][4 * quad : 4 * quad + 4, :].bitcast(I32),
             )
         concept_pool = [load_concepts(j) for j in range(PACK)]
-        value_pool = [load_values(t) for t in range(PACK)]
+        value_pool = [load_values(t) for t in range(PACK - 1)]
+        last_values = last.tile([P, T], F32, name="last_values", align_bytes=64, offset=0)
+        nc.sync.dma_start(last_values[:], vals.rearrange("(p t) n -> t p n", t=PACK)[PACK - 1])
+        value_pool.append(last_values)
 
-        rows_turned = psum.tile([P, 2, 2, P], F32, name="rows_turned", tag="bank5")
+        rows_turned = psum.tile([P, 2, 2, P], F32, name="rows_turned", tag="bank7")
         for v, cols_tile in enumerate((lam_cols, memq_cols)):
             for c in range(2):
                 nc.tensor.transpose(rows_turned[:, v, c, :], cols_tile[:, c : c + 1].to_broadcast([P, P]), ident[:])
@@ -112,29 +117,28 @@ def tile_attend_withoutconcept_claimants_rowchanges_pl_kernel(
         nc.scalar.activation(concept_listed[:, 0, :], concept_pool[0][:].indirect(picks[:]), ACT.Copy)
         nc.scalar.activation(concept_listed[:, 1, :], concept_pool[1][:].indirect(picks[:]), ACT.Copy)
         nc.vector.tensor_copy(concept_listed[:, 2, :], concept_pool[2][:].indirect(picks[:]))
-        nc.scalar.activation(concept_listed[:, 3, 0 : I // 2], concept_pool[3][:].indirect(picks[:, 0:16]), ACT.Copy)
-        nc.vector.tensor_copy(concept_listed[:, 3, I // 2 : I], concept_pool[3][:].indirect(picks[:, 16:32]))
+        nc.scalar.activation(concept_listed[:, 3, 0:LAST_SPLIT], concept_pool[3][:].indirect(picks[:, 0 : LAST_SPLIT // 16]), ACT.Copy)
+        nc.vector.tensor_copy(concept_listed[:, 3, LAST_SPLIT:I], concept_pool[3][:].indirect(picks[:, LAST_SPLIT // 16 : I // 16]))
 
-        part_turned = psum.tile([P, PACK, P], F32, name="part_turned", tag="bank4")
+        part_turned = psum.tile([P, PACK, P], F32, name="part_turned", tag="bank6")
         for t in range(PACK):
             nc.tensor.transpose(part_turned[:, t, :], part_row[:, t::PACK], ident[:])
         neg_part = sb.tile([P, PACK], F32, name="neg_part", tag="concept_pool0", align_bytes=64)
         nc.scalar.activation(neg_part[:], part_turned[:, :, PART_ROW], ACT.Copy, scale=-1.0)
 
-        def score_bank(tag, codes, scales):
-            bank = psum.tile([P, 2, Q], F32, name="score_bank", tag=tag)
-            for r in range(2):
-                cols = slice(r * P, (r + 1) * P)
-                nc.tensor.matmul_mx(
-                    out=bank[:, r, :], lhsT=codes[:, cols], lhsT_scale=scales[:, cols],
-                    rhs=q_codes[:].bitcast(FP8X4), rhs_scale=q_scales[:], start=True, stop=True,
-                )
-            return bank
+        def score(out, codes, scales):
+            nc.tensor.matmul_mx(
+                out=out, lhsT=codes, lhsT_scale=scales,
+                rhs=q_codes[:].bitcast(FP8X4), rhs_scale=q_scales[:], start=True, stop=True,
+            )
 
         key_banks = []
         for half in range(2):
-            cols = slice(2 * half * P, (2 * half + 2) * P)
-            key_banks.append(score_bank("bank%d" % half, key_words[:, cols].bitcast(FP4X4), key_scales[:, cols]))
+            bank = psum.tile([P, 2, Q], F32, name="key_bank", tag="bank%d" % half)
+            for r in range(2):
+                cols = slice((2 * half + r) * P, (2 * half + r + 1) * P)
+                score(bank[:, r, :], key_words[:, cols].bitcast(FP4X4), key_scales[:, cols])
+            key_banks.append(bank)
 
         concept_banks = []
         dealt = concept_listed[:].rearrange("p j (a i t) -> p a j i t", i=2, t=PACK)
@@ -143,13 +147,16 @@ def tile_attend_withoutconcept_claimants_rowchanges_pl_kernel(
             copy = nc.vector.tensor_copy if half == 0 else nc.scalar.copy
             copy(c_grouped[:].rearrange("p t (a i) j -> p a j i t", i=2), dealt[:, :, :, :, 2 * half : 2 * half + 2])
             c_codes, c_scales = quantise("concept%d" % half, c_grouped[:].rearrange("p t m j -> p (t m j)"), 2 * P)
-            concept_banks.append(score_bank("bank%d" % (2 + half), c_codes[:].bitcast(FP8X4), c_scales[:]))
+            for r in range(2):
+                bank = psum.tile([P, Q], F32, name="concept_bank", tag="bank%d" % (2 + 2 * half + r))
+                cols = slice(r * P, (r + 1) * P)
+                score(bank[:], c_codes[:, cols].bitcast(FP8X4), c_scales[:, cols])
+                concept_banks.append(bank)
 
-        key_scores = []
-        for half, (copy, tag) in enumerate(((nc.scalar.copy, "concept_pool3"), (nc.vector.tensor_copy, "concept_grouped1"))):
-            pair_scores = sb.tile([P, 2, Q], F32, name="key_scores%d" % half, tag=tag, align_bytes=64)
-            copy(pair_scores[:], key_banks[half][:])
-            key_scores.append(pair_scores)
+        key_scores = sb.tile([P, PACK, Q], F32, name="key_scores", tag="concept_pool3", align_bytes=64)
+        nc.scalar.copy(key_scores[:, 0:2, :], key_banks[0][:])
+        for r in range(2):
+            nc.vector.tensor_copy(key_scores[:, 2 + r, :], key_banks[1][:, r, :])
 
         inverse_factor = sb.tile([P, PACK], F32, name="inverse_factor", tag="concept_grouped0", align_bytes=64)
         nc.vector.reciprocal(inverse_factor[:], factor[:])
@@ -158,7 +165,7 @@ def tile_attend_withoutconcept_claimants_rowchanges_pl_kernel(
             listed = sb.tile([P, I], BF16, name="value_listed%d" % t)
             nc.scalar.activation(listed[:], value_pool[t][:].indirect(tokens[:]), ACT.Copy)
             words = listed[:].bitcast(F32)
-            turned = psum.tile([P, 2, P], F32, name="value_turned", tag="bank%d" % (4 + t))
+            turned = psum.tile([P, 2, P], F32, name="value_turned", tag="bank%d" % ((6 + t) % 8))
             for u in range(2):
                 nc.tensor.transpose(turned[:, u, :], words[:, u::2], ident[:])
             return turned
@@ -176,7 +183,7 @@ def tile_attend_withoutconcept_claimants_rowchanges_pl_kernel(
             for r in range(2):
                 t = 2 * half + r
                 nc.vector.scalar_tensor_tensor(
-                    scores[:, t, :], concept_banks[half][:, r, :], neg_part[:, t : t + 1], key_scores[half][:, r, :],
+                    scores[:, t, :], concept_banks[t][:], neg_part[:, t : t + 1], key_scores[:, t, :],
                     ALU.mult, ALU.add,
                 )
             scaled = sb.tile([P, 2, Q], F32, name="scaled%d" % half, align_bytes=64)
@@ -184,7 +191,7 @@ def tile_attend_withoutconcept_claimants_rowchanges_pl_kernel(
             nc.scalar.activation(weights[:, pair, :], scaled[:], ACT.Exp)
 
         sums = sb.tile([P, PACK, K], F32, name="sums")
-        denominators = sb.tile([P, K, PACK], F32, name="denominators")
+        denominators = sb.tile([P, PACK, K], F32, name="denominators")
         gains = sb.tile([P, K, PACK], F32, name="gains")
         for half in range(2):
             pair = slice(2 * half, 2 * half + 2)
@@ -193,10 +200,10 @@ def tile_attend_withoutconcept_claimants_rowchanges_pl_kernel(
             )
             for t in (2 * half, 2 * half + 1):
                 nc.vector.tensor_scalar(
-                    denominators[:, :, t], sums[:, t, :], reserve[:, t : t + 1], inverse_factor[:, t : t + 1],
+                    denominators[:, t, :], sums[:, t, :], reserve[:, t : t + 1], inverse_factor[:, t : t + 1],
                     ALU.add, ALU.mult,
                 )
-            nc.vector.reciprocal(gains[:, :, pair], denominators[:, :, pair])
+            nc.vector.reciprocal(gains[:, :, pair].rearrange("p k t -> p t k"), denominators[:, pair, :])
         weight_grouped = sb.tile([P, Q, PACK], BF16, name="weight_grouped", align_bytes=64)
         for h in range(GROUP // RUN):
             nc.vector.tensor_tensor(
@@ -206,21 +213,21 @@ def tile_attend_withoutconcept_claimants_rowchanges_pl_kernel(
                 ALU.mult,
             )
 
-        first_grouped = sb.tile([P, P * PACK], BF16, name="first_grouped", tag="scaled0", align_bytes=64)
-        values = [quantise_values(0, turned[0], first_grouped[:])]
         turned += [gather_values(2), gather_values(3)]
-        second_grouped = sb.tile([P, P * PACK], BF16, name="second_grouped", tag="value_pool2", align_bytes=64)
-        third_grouped = sb.tile([P, P * PACK], BF16, name="third_grouped", align_bytes=64)
-        last_grouped = sb.tile([P, P * PACK], BF16, name="last_grouped", align_bytes=64)
-        values += [quantise_values(1, turned[1], second_grouped[:]), quantise_values(2, turned[2], third_grouped[:])]
-        w_codes, w_scales = quantise(
-            "weight", weight_grouped[:].rearrange("p q t -> p (q t)"), Q, codes_tag="value_pool3"
+        slot = 2 * P * PACK
+        w_codes = last.tile([P, Q], U32, name="weight_codes", align_bytes=64, offset=0)
+        w_scales = sb.tile([P, Q], U8, name="weight_scales", align_bytes=64)
+        nc.vector.quantize_mx(
+            out=w_codes[:].bitcast(FP8X4), scales=w_scales[:], in_=weight_grouped[:].rearrange("p q t -> p (q t)")
         )
-        values.append(quantise_values(3, turned[3], last_grouped[:]))
+        values = []
+        for t in range(PACK):
+            v_grouped = last.tile([P, P * PACK], BF16, name="value_grouped%d" % t, align_bytes=64, offset=(1 + t) * slot)
+            values.append(quantise_values(t, turned[t], v_grouped[:]))
         result = sb.tile([P, PACK, Q], F32, name="result")
         for t in range(PACK):
             v_codes, v_scales = values[t]
-            bank = psum.tile([P, Q], F32, name="result_bank", tag="bank%d" % t)
+            bank = psum.tile([P, Q], F32, name="result_bank", tag="bank%d" % (2 + t))
             nc.tensor.matmul_mx(
                 out=bank[:], lhsT=v_codes[:].bitcast(FP8X4), lhsT_scale=v_scales[:],
                 rhs=w_codes[:].bitcast(FP8X4), rhs_scale=w_scales[:], start=True, stop=True,

from contextlib import ExitStack

import concourse.mybir as mybir
from concourse.masks import make_identity

D, T, I, Q, E, U, GROUP = 512, 2048, 512, 256, 512, 1024, 8
FLOPS = 2 * D * Q * I * 2 + 2 * I * E * Q

F32 = mybir.dt.float32
BF16 = mybir.dt.bfloat16
I32 = mybir.dt.int32
U32 = mybir.dt.uint32
U16 = mybir.dt.uint16
U8 = mybir.dt.uint8
FP8X4 = mybir.dt.float8_e4m3fn_x4
FP4X4 = mybir.dt.float4_e2m1fn_x4
ALU = mybir.AluOpType
ACT = mybir.ActivationFunctionType

P = 128
PACK = 4
K = Q // GROUP
PART_ROW = 16
RUN = 4
CAST_SPLIT = 160
LAST_SPLIT = 288


def tile_attend_withoutconcept_claimants_rowchanges_pl_kernel(
    tc, query, keys_words, keys_scales, concepts, part, lam, sres, slot_factor, vals, memq, offs, offs2,
    out_0, out_1, out_2,
):
    nc = tc.nc
    with ExitStack() as ctx:
        sb = ctx.enter_context(tc.tile_pool(name="sb", bufs=1))
        last = ctx.enter_context(tc.tile_pool(name="last", bufs=1))
        psum = ctx.enter_context(tc.psum_pool(name="psum", bufs=1))

        def quantise(name, grouped, width):
            codes = sb.tile([P, width], U32, name=name + "_codes", align_bytes=64)
            scales = sb.tile([P, width], U8, name=name + "_scales", align_bytes=64)
            nc.vector.quantize_mx(out=codes[:].bitcast(FP8X4), scales=scales[:], in_=grouped)
            return codes, scales

        ident = sb.tile([P, P], F32, name="ident")
        nc.vector.memset(ident[:], 0.0)
        part_pool = sb.tile([P, T], F32, name="part_pool")
        nc.vector.memset(part_pool[:], 0.0)
        key_scale_pool = sb.tile([P, T], U8, name="key_scale_pool")
        nc.gpsimd.memset(key_scale_pool[:].bitcast(I32), 0)
        make_identity(nc, ident[:], nomemset=True)
        shifted = sb.tile([P, PACK, Q], F32, name="shifted")
        nc.scalar.activation(shifted[:, :, 0], ident[:, 0:PACK], ACT.Copy, scale=0.0)

        def load(queue, name, shape, dtype, source):
            tile = sb.tile(shape, dtype, name=name, align_bytes=64)
            queue.dma_start(tile[:], source)
            return tile

        def load_concepts(j):
            return load(nc.sync, "concept_pool%d" % j, [P, U], F32, concepts.rearrange("(p j) u -> j p u", j=PACK)[j])

        def load_values(t):
            return load(nc.sync, "value_pool%d" % t, [P, T], F32, vals.rearrange("(p t) n -> t p n", t=PACK)[t])

        reserve = load(nc.gpsimd, "reserve", [P, PACK], F32, sres.rearrange("(p t) o -> p (t o)", t=PACK))
        factor = load(nc.gpsimd, "factor", [P, PACK], F32, slot_factor.rearrange("o (p t) -> p (o t)", t=PACK))

        tokens = load(nc.sync, "tokens", [P, I // 16], U16, offs)
        picks = load(nc.sync, "picks", [P, I // 16], U16, offs2)
        lam_cols = load(nc.sync, "lam_cols", [P, 2], F32, lam.rearrange("(p c) o -> p (c o)", c=2))
        memq_cols = load(nc.sync, "memq_cols", [P, 2], F32, memq.rearrange("o (p c) -> p (o c)", c=2))
        key_pool = sb.tile([P, T], U16, name="key_pool")
        nc.sync.dma_start(key_pool[:].bitcast(I32), keys_words[0].bitcast(I32))
        query_raw = load(nc.sync, "query_raw", [P, PACK, Q], F32, query.rearrange("(p j) q -> p j q", j=PACK))
        nc.sync.dma_start(part_pool[PART_ROW : PART_ROW + 1, :], part[0:1, :])
        for quad in range(4):
            nc.sync.dma_start(
                key_scale_pool[32 * quad : 32 * quad + 4, :].bitcast(I32),
                keys_scales[0][4 * quad : 4 * quad + 4, :].bitcast(I32),
            )
        concept_pool = [load_concepts(j) for j in range(PACK)]
        value_pool = [load_values(t) for t in range(PACK - 1)]
        last_values = last.tile([P, T], F32, name="last_values", align_bytes=64, offset=0)
        nc.sync.dma_start(last_values[:], vals.rearrange("(p t) n -> t p n", t=PACK)[PACK - 1])
        value_pool.append(last_values)

        rows_turned = psum.tile([P, 2, 2, P], F32, name="rows_turned", tag="bank7")
        for v, cols_tile in enumerate((lam_cols, memq_cols)):
            for c in range(2):
                nc.tensor.transpose(rows_turned[:, v, c, :], cols_tile[:, c : c + 1].to_broadcast([P, P]), ident[:])
        rows = sb.tile([P, 2, Q], F32, name="rows")
        nc.scalar.activation(
            rows[:].rearrange("p v (n c) -> p v n c", c=2), rows_turned[:].rearrange("p v c n -> p v n c"), ACT.Copy
        )

        key_listed = sb.tile([P, I], U16, name="key_listed")
        nc.vector.tensor_copy(key_listed[:], key_pool[:].indirect(tokens[:]))
        query_grouped = sb.tile([P, Q, PACK], BF16, name="query_grouped", align_bytes=64)
        nc.vector.tensor_copy(
            query_grouped[:].rearrange("p (c i) j -> p c j i", i=RUN), query_raw[:].rearrange("p j (c i) -> p c j i", i=RUN)
        )
        key_scales = sb.tile([P, I], U8, name="key_scales", align_bytes=64)
        nc.vector.tensor_copy(
            key_scales[:].rearrange("p (t m) -> p m t", t=PACK), key_scale_pool[:].indirect(tokens[:])
        )
        key_words = sb.tile([P, I], U16, name="key_words", align_bytes=64)
        nc.vector.tensor_copy(
            key_words[:].rearrange("p (t m) -> p m t", t=PACK), key_listed[:].rearrange("p (m t) -> p m t", t=PACK)
        )
        q_codes, q_scales = quantise("query", query_grouped[:].rearrange("p q j -> p (q j)"), Q)

        part_row = sb.tile([P, I], F32, name="part_row")
        nc.scalar.activation(part_row[:], part_pool[:].indirect(tokens[:]), ACT.Copy)

        concept_listed = sb.tile([P, PACK, I], BF16, name="concept_listed")
        nc.scalar.activation(concept_listed[:, 0, :], concept_pool[0][:].indirect(picks[:]), ACT.Copy)
        nc.scalar.activation(concept_listed[:, 1, :], concept_pool[1][:].indirect(picks[:]), ACT.Copy)
        nc.vector.tensor_copy(concept_listed[:, 2, :], concept_pool[2][:].indirect(picks[:]))
        nc.scalar.activation(concept_listed[:, 3, 0:LAST_SPLIT], concept_pool[3][:].indirect(picks[:, 0 : LAST_SPLIT // 16]), ACT.Copy)
        nc.vector.tensor_copy(concept_listed[:, 3, LAST_SPLIT:I], concept_pool[3][:].indirect(picks[:, LAST_SPLIT // 16 : I // 16]))

        part_turned = psum.tile([P, PACK, P], F32, name="part_turned", tag="bank6")
        for t in range(PACK):
            nc.tensor.transpose(part_turned[:, t, :], part_row[:, t::PACK], ident[:])
        neg_part = sb.tile([P, PACK], F32, name="neg_part", tag="concept_pool0", align_bytes=64)
        nc.scalar.activation(neg_part[:], part_turned[:, :, PART_ROW], ACT.Copy, scale=-1.0)

        def score(out, codes, scales):
            nc.tensor.matmul_mx(
                out=out, lhsT=codes, lhsT_scale=scales,
                rhs=q_codes[:].bitcast(FP8X4), rhs_scale=q_scales[:], start=True, stop=True,
            )

        key_banks = []
        for half in range(2):
            bank = psum.tile([P, 2, Q], F32, name="key_bank", tag="bank%d" % half)
            for r in range(2):
                cols = slice((2 * half + r) * P, (2 * half + r + 1) * P)
                score(bank[:, r, :], key_words[:, cols].bitcast(FP4X4), key_scales[:, cols])
            key_banks.append(bank)

        concept_banks = []
        dealt = concept_listed[:].rearrange("p j (a i t) -> p a j i t", i=2, t=PACK)
        for half in range(2):
            c_grouped = sb.tile([P, 2, P, PACK], BF16, name="concept_grouped%d" % half, align_bytes=64)
            copy = nc.vector.tensor_copy if half == 0 else nc.scalar.copy
            copy(c_grouped[:].rearrange("p t (a i) j -> p a j i t", i=2), dealt[:, :, :, :, 2 * half : 2 * half + 2])
            c_codes, c_scales = quantise("concept%d" % half, c_grouped[:].rearrange("p t m j -> p (t m j)"), 2 * P)
            for r in range(2):
                bank = psum.tile([P, Q], F32, name="concept_bank", tag="bank%d" % (2 + 2 * half + r))
                cols = slice(r * P, (r + 1) * P)
                score(bank[:], c_codes[:, cols].bitcast(FP8X4), c_scales[:, cols])
                concept_banks.append(bank)

        key_scores = sb.tile([P, PACK, Q], F32, name="key_scores", tag="concept_pool3", align_bytes=64)
        nc.scalar.copy(key_scores[:, 0:2, :], key_banks[0][:])
        for r in range(2):
            nc.vector.tensor_copy(key_scores[:, 2 + r, :], key_banks[1][:, r, :])

        inverse_factor = sb.tile([P, PACK], F32, name="inverse_factor", tag="concept_grouped0", align_bytes=64)
        nc.vector.reciprocal(inverse_factor[:], factor[:])

        def gather_values(t):
            listed = sb.tile([P, I], BF16, name="value_listed%d" % t)
            nc.scalar.activation(listed[:], value_pool[t][:].indirect(tokens[:]), ACT.Copy)
            words = listed[:].bitcast(F32)
            turned = psum.tile([P, 2, P], F32, name="value_turned", tag="bank%d" % ((6 + t) % 8))
            for u in range(2):
                nc.tensor.transpose(turned[:, u, :], words[:, u::2], ident[:])
            return turned

        def quantise_values(t, turned, v_grouped):
            nc.scalar.copy(v_grouped.bitcast(F32).rearrange("p (e u) -> p e u", u=2), turned[:].rearrange("p u e -> p e u"))
            return quantise("value%d" % t, v_grouped, P)

        turned = [gather_values(0), gather_values(1)]

        scores = sb.tile([P, PACK, Q], F32, name="scores")
        weights = sb.tile([P, PACK, Q], F32, name="weights", tag="value_pool1", align_bytes=64)
        for half in range(2):
            pair = slice(2 * half, 2 * half + 2)
            for r in range(2):
                t = 2 * half + r
                nc.vector.scalar_tensor_tensor(
                    scores[:, t, :], concept_banks[t][:], neg_part[:, t : t + 1], key_scores[:, t, :],
                    ALU.mult, ALU.add,
                )
            scaled = sb.tile([P, 2, Q], F32, name="scaled%d" % half, align_bytes=64)
            nc.vector.tensor_tensor(scaled[:], scores[:, pair, :], rows[:, 0:1, :].to_broadcast([P, 2, Q]), ALU.mult)
            nc.scalar.activation(weights[:, pair, :], scaled[:], ACT.Exp)

        sums = sb.tile([P, PACK, K], F32, name="sums")
        denominators = sb.tile([P, PACK, K], F32, name="denominators")
        gains = sb.tile([P, K, PACK], F32, name="gains")
        for half in range(2):
            pair = slice(2 * half, 2 * half + 2)
            nc.vector.tensor_reduce(
                sums[:, pair, :], weights[:, pair, :].rearrange("p t (k j) -> p t k j", j=GROUP), mybir.AxisListType.X, ALU.add
            )
            for t in (2 * half, 2 * half + 1):
                nc.vector.tensor_scalar(
                    denominators[:, t, :], sums[:, t, :], reserve[:, t : t + 1], inverse_factor[:, t : t + 1],
                    ALU.add, ALU.mult,
                )
            nc.vector.reciprocal(gains[:, :, pair].rearrange("p k t -> p t k"), denominators[:, pair, :])
        weight_grouped = sb.tile([P, Q, PACK], BF16, name="weight_grouped", align_bytes=64)
        for h in range(GROUP // RUN):
            nc.vector.tensor_tensor(
                weight_grouped[:].rearrange("p (k h i) t -> p h k t i", k=K, i=RUN)[:, h],
                weights[:].rearrange("p t (k h i) -> p h k t i", k=K, i=RUN)[:, h],
                gains[:].unsqueeze(3).to_broadcast([P, K, PACK, RUN]),
                ALU.mult,
            )

        turned += [gather_values(2), gather_values(3)]
        slot = 2 * P * PACK
        w_codes = last.tile([P, Q], U32, name="weight_codes", align_bytes=64, offset=0)
        w_scales = sb.tile([P, Q], U8, name="weight_scales", align_bytes=64)
        nc.vector.quantize_mx(
            out=w_codes[:].bitcast(FP8X4), scales=w_scales[:], in_=weight_grouped[:].rearrange("p q t -> p (q t)")
        )
        values = []
        for t in range(PACK):
            v_grouped = last.tile([P, P * PACK], BF16, name="value_grouped%d" % t, align_bytes=64, offset=(1 + t) * slot)
            values.append(quantise_values(t, turned[t], v_grouped[:]))
        result = sb.tile([P, PACK, Q], F32, name="result")
        for t in range(PACK):
            v_codes, v_scales = values[t]
            bank = psum.tile([P, Q], F32, name="result_bank", tag="bank%d" % (2 + t))
            nc.tensor.matmul_mx(
                out=bank[:], lhsT=v_codes[:].bitcast(FP8X4), lhsT_scale=v_scales[:],
                rhs=w_codes[:].bitcast(FP8X4), rhs_scale=w_scales[:], start=True, stop=True,
            )
            nc.vector.tensor_tensor(shifted[:, t, 1:Q], bank[:, 0 : Q - 1], rows[:, 1, 1:Q], ALU.mult)
            nc.vector.tensor_tensor(result[:, t, :], bank[:], shifted[:, t, :], ALU.subtract)
            nc.sync.dma_start(out_0.rearrange("(p t) q -> t p q", t=PACK)[t], result[:, t, :])

        result_grouped = sb.tile([P, Q, PACK], BF16, name="result_grouped", align_bytes=64)
        for copy, cols in ((nc.vector.tensor_copy, slice(0, CAST_SPLIT)), (nc.scalar.copy, slice(CAST_SPLIT, Q))):
            copy(
                result_grouped[:, cols, :].rearrange("p (c i) t -> p c t i", i=RUN),
                result[:, :, cols].rearrange("p t (c i) -> p c t i", i=RUN),
            )
        y_codes, y_scales = quantise("result", result_grouped[:].rearrange("p q t -> p (q t)"), Q)
        nc.sync.dma_start(out_1[0].rearrange("p c r -> p (c r)").bitcast(I32), y_codes[:].bitcast(I32))
        for quad in range(4):
            queue = nc.scalar if quad % 2 == 0 else nc.sync
            queue.dma_start(
                out_2[0][4 * quad : 4 * quad + 4, :].bitcast(I32), y_scales[32 * quad : 32 * quad + 4, :].bitcast(I32)
            )
